import numpy as np
import ml_dtypes


def mxq(x, axis, fmt="e4m3"):
    dtype, down = {"e4m3": (ml_dtypes.float8_e4m3fn, 7), "e5m2": (ml_dtypes.float8_e5m2, 14)}[fmt]
    v = np.moveaxis(np.asarray(x, np.float32).astype(ml_dtypes.bfloat16).astype(np.float64), axis, -1)
    blocks = v.reshape(v.shape[:-1] + (-1, 32))
    amax = np.abs(blocks).max(-1, keepdims=True)
    byte = np.maximum(np.where(amax > 0, np.frexp(amax)[1] - 1 + 127, 0) - down, 1)
    scale = np.exp2(byte - 127.0)
    codes = (blocks / scale).astype(np.float32).astype(dtype).astype(np.float64)
    return np.moveaxis((codes * scale).reshape(v.shape), -1, axis)


WIDE = False


def mx_kscale(k):
    if not WIDE:
        return np.ones(k)
    levels = np.array([10, -10, 5, -5, 0])
    if k % 512:
        return np.exp2(np.random.permutation(np.resize(levels, k // 32))).repeat(32)
    a = np.empty((k // 512, 16))
    for p in range(k // 512):
        a[p, :8] = np.random.permutation(np.resize(levels, 8))
        for g in range(8):
            far = levels[np.abs(levels - a[p, g]) >= 10]
            a[p, g + 8] = far[np.random.randint(len(far))]
    return np.exp2(a.ravel()).repeat(32)


BF16 = ml_dtypes.bfloat16


def bf(x):
    return np.asarray(x, np.float32).astype(BF16)


def f64(x):
    return np.asarray(x).astype(np.float64)


E2M1 = np.array([0.0, 0.5, 1.0, 1.5, 2.0, 3.0, 4.0, 6.0, -0.0, -0.5, -1.0, -1.5, -2.0, -3.0, -4.0, -6.0])


def pack_weight(w, fmt):
    k, n = w.shape
    w = f64(bf(w)).reshape(k // 32, 32, n)
    amax = np.abs(w).max(1)
    if fmt == "e4m3":
        byte = np.frexp(amax)[1] - 1 + 127 - 7
    else:
        mant, ex = np.frexp(amax / 6.0)
        byte = np.where(mant > 0.5, ex, ex - 1) + 127
    byte = np.clip(np.where(amax > 0, byte, 1), 1, 254)
    scaled = (w * np.exp2(127.0 - byte)[:, None, :]).reshape(k, n).astype(np.float32)
    by_word = np.ascontiguousarray(scaled.reshape(k // 512, 128, 4, n).transpose(0, 1, 3, 2))
    if fmt == "e4m3":
        words = by_word.astype(ml_dtypes.float8_e4m3fn).view(np.uint8)
    else:
        c = by_word.astype(ml_dtypes.float4_e2m1fn).view(np.uint8) & 0xF
        words = c[..., 0::2] | (c[..., 1::2] << 4)
    return np.ascontiguousarray(words), np.ascontiguousarray(byte.astype(np.uint8).reshape(k // 512, 16, n))


def unpack_weight(words, scales, fmt):
    g, p, n, _ = words.shape
    if fmt == "e4m3":
        vals = np.ascontiguousarray(words).view(ml_dtypes.float8_e4m3fn).astype(np.float64)
    else:
        nib = np.empty((g, p, n, 4), np.uint8)
        nib[..., 0::2] = words & 0xF
        nib[..., 1::2] = words >> 4
        vals = E2M1[nib]
    vals = vals * np.repeat(np.exp2(scales.astype(np.float64) - 127.0), 8, axis=1)[..., None]
    return vals.transpose(0, 1, 3, 2).reshape(g * 512, n)
def pack4(w):
    words, scales = pack_weight(w, "e2m1")
    return words.reshape(words.shape[0], 128, -1), scales


def unpack4(words, scales):
    return unpack_weight(words.reshape(words.shape[0], 128, -1, 2), scales, "e2m1")


E4M3FN = np.array([(-1.0 if i & 128 else 1.0) * ((1.0 + (i & 7) / 8.0) * 2.0 ** (((i >> 3) & 15) - 7) if i & 120 else (i & 7) * 2.0 ** -9) for i in range(256)])


def e4m3fn_bytes(y):
    return np.clip(np.asarray(y, np.float64), -448.0, 448.0).astype(np.float32).astype(ml_dtypes.float8_e4m3fn).view(np.uint8)


def e4m3fn_values(b):
    return E4M3FN[b]

def planes(Y):
    n, m = Y.shape
    b = f64(bf(Y)).reshape(n // 32, 32, m)
    amax = np.abs(b).max(1)
    byte = np.clip(np.where(amax > 0, np.frexp(amax)[1] - 1 + 127 - 7, 1), 1, 254)
    codes = (b * np.exp2(127.0 - byte)[:, None, :]).reshape(n, m).astype(np.float32).astype(ml_dtypes.float8_e4m3fn).view(np.uint8)
    words = codes.reshape(n // 512, 128, 4, m).transpose(0, 1, 3, 2)
    return np.ascontiguousarray(words), np.ascontiguousarray(byte.astype(np.uint8).reshape(n // 512, 16, m))


E, T, D, F = 5, 256, 1024, 1536

def setup_inputs():
    ks = mx_kscale(D)
    kh = mx_kscale(F)
    S = np.random.randn(E, T, D) * ks
    S_scale = (np.abs(S).max(axis=1, keepdims=True) / 448.0).astype(np.float32)
    S_bytes = e4m3fn_bytes(S / f64(S_scale))
    U = (1.0 + 0.5 * np.random.randn(T, F)) * kh
    W1 = 1.5 * np.random.randn(E, D, F) / np.sqrt(D) / ks[None, :, None]
    W2 = np.random.randn(E, F, D) / np.sqrt(F) / kh[None, :, None]
    W1_words, W1_scales = pack4(W1.reshape(E * D, F))
    W2_words, W2_scales = pack4(W2.reshape(E * F, D))
    r = np.exp(0.8 * np.random.randn(D))
    skip_gain = r * (1.0 + 0.1 * np.random.randn(D)) / ks
    delta_gain = 0.8 * r * (1.0 + 0.1 * np.random.randn(E, D))
    delta_bias = 0.3 * r * np.random.randn(E, D)
    return {"S_bytes": S_bytes, "S_scale": S_scale, "U": bf(U),
            "W1_words": W1_words, "W1_scales": W1_scales,
            "W2_words": W2_words, "W2_scales": W2_scales,
            "skip_gain": bf(skip_gain), "delta_gain": bf(delta_gain), "delta_bias": bf(delta_bias)}

def reference(S_bytes, S_scale, U, W1_words, W1_scales, W2_words, W2_scales, skip_gain, delta_gain, delta_bias):
    S = e4m3fn_values(S_bytes) * np.repeat(f64(S_scale), T, axis=1)
    W1 = unpack4(W1_words, W1_scales).reshape(E, D, F)
    W2 = unpack4(W2_words, W2_scales).reshape(E, F, D)
    Z = mxq(S, 2, "e4m3") @ W1
    H = Z / (1.0 + np.exp(-Z)) * f64(U)
    O = mxq(H, 2, "e4m3") @ W2
    y = S * f64(skip_gain) + O * f64(delta_gain)[:, None, :] + f64(delta_bias)[:, None, :]
    Y = y.reshape(E * T, D).T
    words, scales = planes(Y)
    return y, words, scales

@@ -1,0 +1,435 @@
+from contextlib import ExitStack
+
+import concourse.mybir as mybir
+from concourse.masks import make_identity
+
+E, T, D, F = 5, 256, 1024, 1536
+FLOPS = 2 * E * T * D * F * 2
+
+F32 = mybir.dt.float32
+BF16 = mybir.dt.bfloat16
+I32 = mybir.dt.int32
+U32 = mybir.dt.uint32
+U8 = mybir.dt.uint8
+FP8 = mybir.dt.float8_e4m3fn
+FP8X4 = mybir.dt.float8_e4m3fn_x4
+FP4X4 = mybir.dt.float4_e2m1fn_x4
+ACT = mybir.ActivationFunctionType
+ALU = mybir.AluOpType
+
+P = 128
+PACK = 4
+K_PASS = P * PACK
+BANK = 512
+N_BANKS = 8
+TILES = T // P
+N_TILES = E * TILES
+D_PASSES = D // K_PASS
+F_PASSES = F // K_PASS
+N_UNITS = E * D_PASSES
+QUADS = 4
+SCALE_SLOTS = 2
+EARLY_TILES = N_TILES - TILES
+
+
+def tile_ensemble_rollout_step_b12_kernel(
+    tc, S_bytes, S_scale, U, W1_words, W1_scales, W2_words, W2_scales, skip_gain, delta_gain, delta_bias,
+    out_0, out_1, out_2,
+):
+    nc = tc.nc
+    with ExitStack() as ctx:
+        keep = ctx.enter_context(tc.tile_pool(name="keep", bufs=1))
+        work = ctx.enter_context(tc.tile_pool(name="work", bufs=2))
+        psum = ctx.enter_context(tc.psum_pool(name="psum", bufs=1))
+        ctx.enter_context(tc.manual_schedule())
+
+        banks = [psum.tile([P, BANK], F32, name=f"bank{b}") for b in range(N_BANKS)]
+        free = list(range(N_BANKS))
+
+        def next_bank():
+            b = free[0]
+            free.remove(b)
+            return b
+
+        ident = keep.tile([P, P], F32)
+        zero_in = keep.tile([P, 1], F32)
+        zero = keep.tile([P, 1], F32)
+        s_bytes = [keep.tile([P, TILES, K_PASS], U8, name=f"s_bytes{u}") for u in range(N_UNITS)]
+        w1 = [keep.tile([P, D_PASSES, 2 * F], U8, name=f"w1_{e}", align_bytes=64) for e in range(E)]
+        w2 = [keep.tile([P, F_PASSES, 2 * D], U8, name=f"w2_{e}", align_bytes=64) for e in range(E)]
+        w1_sc = [keep.tile([P, D_PASSES, F], U8, name=f"w1_sc{s}", align_bytes=64) for s in range(SCALE_SLOTS)]
+        w2_sc = [keep.tile([P, F_PASSES, D], U8, name=f"w2_sc{s}", align_bytes=64) for s in range(SCALE_SLOTS)]
+        gain = [keep.tile([P, D], BF16, name=f"gain{e}") for e in range(E)]
+        u_rows = keep.tile([P, TILES, F], BF16)
+        u_t = keep.tile([P, F_PASSES, T, PACK], BF16)
+        u_sorted = keep.tile([P, TILES, F // 2], F32)
+        scale = [keep.tile([P, D_PASSES, PACK], F32, name=f"scale{e}") for e in range(E)]
+        bias = [keep.tile([P, D_PASSES, PACK], BF16, name=f"bias{e}") for e in range(E)]
+        skip_scale = [keep.tile([P, D_PASSES, PACK], F32, name=f"skip_scale{e}") for e in range(E)]
+        skip = keep.tile([P, D_PASSES, PACK], BF16)
+        y_sc_early = keep.tile([P, D_PASSES, EARLY_TILES * P], U8, align_bytes=64)
+        y_sc_late = keep.tile([P, D_PASSES, TILES * P], U8, align_bytes=64)
+
+        def by_word(row):
+            return row.rearrange("(g p t) -> p g t", p=P, t=PACK)
+
+        def load_scale(e):
+            nc.sync.dma_start(out=scale[e][:], in_=by_word(S_scale[e, 0]))
+
+        def load_bias(e):
+            nc.sync.dma_start(out=bias[e][:], in_=by_word(delta_bias[e]))
+
+        def load_member_s(e):
+            for g in range(D_PASSES):
+                load_s(e * D_PASSES + g)
+            load_scale(e)
+            load_bias(e)
+
+        def join_skip(e):
+            nc.vector.tensor_tensor(out=skip_scale[e][:], in0=scale[e][:], in1=skip[:], op=ALU.mult)
+
+        def load_s(u):
+            e, g = divmod(u, D_PASSES)
+            nc.sync.dma_start(
+                out=s_bytes[u][:], in_=S_bytes[e].rearrange("(tt p) (g k) -> g p tt k", p=P, k=K_PASS)[g]
+            )
+
+        def load_weights(words_tile, scale_tile, words, scales, e, passes):
+            rows = slice(e * passes, (e + 1) * passes)
+            for q in range(QUADS):
+                nc.sync.dma_start(
+                    out=scale_tile[32 * q : 32 * q + 4].bitcast(I32),
+                    in_=scales[rows, 4 * q : 4 * q + 4, :].rearrange("g r n -> r g n").bitcast(I32),
+                )
+            nc.sync.dma_start(out=words_tile[:].bitcast(I32), in_=words[rows].rearrange("g p n -> p g n").bitcast(I32))
+
+        def load_w1(e):
+            load_weights(w1[e], w1_sc[e % SCALE_SLOTS], W1_words, W1_scales, e, D_PASSES)
+
+        def load_w2(e):
+            load_weights(w2[e], w2_sc[e % SCALE_SLOTS], W2_words, W2_scales, e, F_PASSES)
+            nc.sync.dma_start(out=gain[e][:], in_=delta_gain[e].partition_broadcast(P))
+
+        wide, v_bank, s_bf, s_codes, s_sc, skip_t = {}, {}, {}, {}, {}, {}
+        silu, h_bf, h_codes, h_sc, y, y_bf, y_t = {}, {}, {}, {}, {}, {}, {}
+
+        def widen(u, on_vector=False):
+            wide[u] = work.tile([P, TILES * K_PASS], BF16, name="wide", bufs=3)
+            codes = s_bytes[u][:].rearrange("p tt k -> p (tt k)").bitcast(FP8)
+            if on_vector:
+                nc.vector.tensor_copy(out=wide[u][:], in_=codes)
+            else:
+                nc.scalar.copy(out=wide[u][:], in_=codes)
+
+        def turn_pairs(bank, words_of):
+            for half in range(2):
+                for tt in range(TILES):
+                    col = half * T + tt * P
+                    nc.tensor.transpose(bank[:, col : col + P], words_of(tt)[:, half : K_PASS // 2 : 2], ident[:])
+
+        def turn_s(u):
+            v_bank[u] = next_bank()
+            words = wide[u][:].bitcast(F32)
+            turn_pairs(banks[v_bank[u]], lambda tt: words[:, tt * (K_PASS // 2) : (tt + 1) * (K_PASS // 2)])
+
+        def scale_s(u, first=0, last=T):
+            e, g = divmod(u, D_PASSES)
+            if first == 0:
+                s_bf[u] = work.tile([P, T * PACK], BF16, name="s_bf", bufs=2, align_bytes=64)
+            nc.vector.tensor_tensor(
+                out=s_bf[u][:].rearrange("p (m h b) -> p m h b", h=2, b=2)[:, first:last],
+                in0=banks[v_bank[u]][:].bitcast(BF16).rearrange("p (h m b) -> p m h b", h=2, b=2)[:, first:last],
+                in1=scale[e][:, g, :].rearrange("p (h b) -> p h b", b=2).unsqueeze(1).to_broadcast([P, last - first, 2, 2]),
+                op=ALU.mult,
+            )
+
+        def quantize_s(u, first=0, last=T):
+            if first == 0:
+                s_codes[u] = work.tile([P, T], U32, name="s_codes", bufs=4, align_bytes=64)
+                s_sc[u] = work.tile([P, T], U8, name="s_sc", bufs=4, align_bytes=64)
+            nc.vector.quantize_mx(
+                out=s_codes[u][:, first:last].bitcast(FP8X4),
+                scales=s_sc[u][:, first:last],
+                in_=s_bf[u][:, first * PACK : last * PACK],
+            )
+
+        def skip_term(u):
+            e, g = divmod(u, D_PASSES)
+            skip_t[u] = work.tile([P, PACK, T], F32, name="skip_t", bufs=6)
+            values = banks[v_bank[u]][:].bitcast(BF16).rearrange("p (h m b) -> p h b m", h=2, b=2)
+            for t in range(PACK):
+                nc.scalar.activation(
+                    out=skip_t[u][:, t, :], in_=values[:, t // 2, t % 2, :], func=ACT.Identity,
+                    bias=bias[e][:, g, t : t + 1], scale=skip_scale[e][:, g, t : t + 1],
+                )
+
+        def first_product(i):
+            e, tt = divmod(i, TILES)
+            cols = slice(tt * P, (tt + 1) * P)
+            for c in range(F_PASSES):
+                b = next_bank()
+                bank = banks[b]
+                for g in range(D_PASSES):
+                    u = e * D_PASSES + g
+                    nc.tensor.matmul_mx(
+                        out=bank[:],
+                        lhsT=s_codes[u][:, cols].bitcast(FP8X4),
+                        lhsT_scale=s_sc[u][:, cols],
+                        rhs=w1[e][:, g, 2 * c * BANK : 2 * (c + 1) * BANK].bitcast(FP4X4),
+                        rhs_scale=w1_sc[e % SCALE_SLOTS][:, g, c * BANK : (c + 1) * BANK],
+                        start=(g == 0),
+                        stop=(g == D_PASSES - 1),
+                    )
+                silu[i, c] = work.tile([P, PACK, P], F32, name="silu", bufs=6)
+                nc.scalar.activation(
+                    out=silu[i, c][:], in_=bank[:].rearrange("p (m t) -> p t m", t=PACK), func=ACT.Silu, bias=zero[:]
+                )
+                free.append(b)
+
+        def turn_planes(bank, plane_of):
+            for t in range(PACK):
+                nc.tensor.transpose(bank[:, t * P : (t + 1) * P], plane_of(t), ident[:])
+
+        def modulate(i):
+            tt = i % TILES
+            h_bf[i] = work.tile([P, F_PASSES, K_PASS], BF16, name="h_bf", align_bytes=64)
+            h_codes[i] = work.tile([P, F_PASSES * P], U32, name="h_codes", align_bytes=64)
+            h_sc[i] = work.tile([P, F_PASSES * P], U8, name="h_sc", align_bytes=64)
+            for c in range(F_PASSES):
+                b = next_bank()
+                bank = banks[b]
+                turn_planes(bank, lambda t: silu[i, c][:, t, :])
+                nc.vector.tensor_tensor(
+                    out=h_bf[i][:, c, :].rearrange("p (m t) -> p m t", t=PACK),
+                    in0=bank[:].rearrange("p (t m) -> p m t", t=PACK),
+                    in1=u_t[:, c, tt * P : (tt + 1) * P, :],
+                    op=ALU.mult,
+                )
+                free.append(b)
+
+        def quantize_h(i, first, last):
+            cols = slice(first * P, last * P)
+            nc.vector.quantize_mx(
+                out=h_codes[i][:, cols].bitcast(FP8X4),
+                scales=h_sc[i][:, cols],
+                in_=h_bf[i][:, first:last, :].rearrange("p c k -> p (c k)"),
+            )
+
+        def second_product(i, g):
+            e = i // TILES
+            if g == 0:
+                y[i] = work.tile([P, D], F32, name="y", bufs=4)
+            cols = slice(g * BANK, (g + 1) * BANK)
+            b = next_bank()
+            bank = banks[b]
+            for c in range(F_PASSES):
+                nc.tensor.matmul_mx(
+                    out=bank[:],
+                    lhsT=h_codes[i][:, c * P : (c + 1) * P].bitcast(FP8X4),
+                    lhsT_scale=h_sc[i][:, c * P : (c + 1) * P],
+                    rhs=w2[e][:, c, 2 * g * BANK : 2 * (g + 1) * BANK].bitcast(FP4X4),
+                    rhs_scale=w2_sc[e % SCALE_SLOTS][:, c, cols],
+                    start=(c == 0),
+                    stop=(c == F_PASSES - 1),
+                )
+            nc.vector.tensor_tensor(out=y[i][:, cols], in0=bank[:], in1=gain[e][:, cols], op=ALU.mult)
+            free.append(b)
+
+        def turn_skip(i, g):
+            e, tt = divmod(i, TILES)
+            b = next_bank()
+            turn_planes(banks[b], lambda t: skip_t[e * D_PASSES + g][:, t, tt * P : (tt + 1) * P])
+            return b
+
+        def add_skip(i, g, b):
+            part = y[i][:, g * BANK : (g + 1) * BANK].rearrange("p (m t) -> p m t", t=PACK)
+            nc.vector.tensor_tensor(out=part, in0=banks[b][:].rearrange("p (t m) -> p m t", t=PACK), in1=part, op=ALU.add)
+            free.append(b)
+
+        def store_y(i, first=0, last=D_PASSES):
+            e, tt = divmod(i, TILES)
+            cols = slice(first * K_PASS, last * K_PASS)
+            nc.sync.dma_start(out=out_0[e, tt * P : (tt + 1) * P, cols], in_=y[i][:, cols])
+
+        def round_y(i, first=0, last=D_PASSES, copy=nc.scalar.copy):
+            y_bf[i, first] = work.tile([P, (last - first) * K_PASS], BF16, name="y_bf", bufs=3)
+            copy(
+                out=y_bf[i, first][:].rearrange("p (g h m b) -> p g h m b", m=P, h=2, b=2),
+                in_=y[i][:, first * K_PASS : last * K_PASS].rearrange("p (g m h b) -> p g h m b", m=P, h=2, b=2),
+            )
+
+        def turn_y(i, first=0, last=D_PASSES):
+            b = next_bank()
+            bank = banks[b]
+            words = y_bf[i, first][:].bitcast(F32)
+            for j in range(2 * (last - first)):
+                nc.tensor.transpose(bank[:, j * P : (j + 1) * P], words[:, j * P : (j + 1) * P], ident[:])
+            y_t[i, first] = work.tile([P, (last - first) * K_PASS], BF16, name="y_t", bufs=3, align_bytes=64)
+            nc.scalar.copy(
+                out=y_t[i, first][:].bitcast(F32).rearrange("p (g m h) -> p g m h", m=P, h=2),
+                in_=bank[:, : 2 * (last - first) * P].rearrange("p (g h m) -> p g m h", m=P, h=2),
+            )
+            free.append(b)
+
+        def store_scales(plane, first, count):
+            for q in range(QUADS):
+                nc.sync.dma_start(
+                    out=out_2[:, 4 * q : 4 * q + 4, first * P : (first + count) * P].rearrange("g r m -> r g m").bitcast(I32),
+                    in_=plane[32 * q : 32 * q + 4].bitcast(I32),
+                )
+
+        def quantize_y(i, first=0, last=D_PASSES):
+            y_codes = work.tile([P, last - first, P], U32, name="y_codes", bufs=4, align_bytes=64)
+            plane, at = (y_sc_early, i) if i < EARLY_TILES else (y_sc_late, i - EARLY_TILES)
+            for g in range(first, last):
+                nc.vector.quantize_mx(
+                    out=y_codes[:, g - first, :].bitcast(FP8X4),
+                    scales=plane[:, g, at * P : (at + 1) * P],
+                    in_=y_t[i, first][:, (g - first) * K_PASS : (g - first + 1) * K_PASS],
+                )
+            nc.sync.dma_start(
+                out=out_1[first:last, :, i * P : (i + 1) * P, :].rearrange("g p m t -> p g (m t)").bitcast(I32),
+                in_=y_codes[:].bitcast(I32),
+            )
+
+        make_identity(nc, ident[:])
+        nc.vector.memset(zero_in[:], 0.0)
+        nc.scalar.activation(out=zero[:], in_=zero_in[:], func=ACT.Silu)
+        for s in range(SCALE_SLOTS):
+            nc.vector.memset(w1_sc[s][:].bitcast(I32), 0)
+            nc.vector.memset(w2_sc[s][:].bitcast(I32), 0)
+        load_s(0)
+        load_s(1)
+        load_scale(0)
+        nc.sync.dma_start(out=skip[:], in_=by_word(skip_gain))
+        load_bias(0)
+        load_w1(0)
+        nc.sync.dma_start(out=u_rows[:], in_=U.rearrange("(tt p) f -> p tt f", p=P))
+        load_member_s(1)
+        load_w2(0)
+        load_member_s(2)
+        load_w1(1)
+        load_w2(1)
+
+        def turn_u():
+            for c in range(F_PASSES):
+                b = next_bank()
+                for half in range(2):
+                    for tt in range(TILES):
+                        col, word = half * T + tt * P, (2 * c + half) * P
+                        nc.tensor.transpose(banks[b][:, col : col + P], u_sorted[:, tt, word : word + P], ident[:])
+                nc.scalar.copy(
+                    out=u_t[:, c].rearrange("p m t -> p (m t)").bitcast(F32).rearrange("p (m h) -> p m h", h=2),
+                    in_=banks[b][:].rearrange("p (h m) -> p m h", h=2),
+                )
+                free.append(b)
+
+        def finish_unit(u):
+            skip_term(u)
+            free.append(v_bank[u])
+
+        widen(0, on_vector=True)
+        widen(1)
+        turn_s(0)
+        turn_s(1)
+        join_skip(0)
+        for u in range(D_PASSES):
+            scale_s(u, 0, P)
+            skip_term(u)
+        for u in range(D_PASSES):
+            quantize_s(u, 0, P)
+        first_product(0)
+        scale_s(0, P, T)
+        nc.vector.tensor_copy(
+            out=u_sorted[:].rearrange("p tt (c h m) -> p (tt c) h m", h=2, m=P),
+            in_=u_rows[:].bitcast(F32).rearrange("p tt (c m h) -> p (tt c) h m", h=2, m=P),
+        )
+        scale_s(1, P, T)
+        free.extend(v_bank[u] for u in range(D_PASSES))
+        for u in range(D_PASSES):
+            quantize_s(u, P, T)
+        widen(2, on_vector=True)
+        widen(3, on_vector=True)
+        join_skip(1)
+        turn_u()
+        modulate(0)
+        first_product(1)
+        quantize_h(0, 0, 2)
+        widen(4, on_vector=True)
+        quantize_h(0, 2, 3)
+        for u in (2, 3):
+            turn_s(u)
+            scale_s(u)
+        for u in (2, 3):
+            quantize_s(u)
+            finish_unit(u)
+        load_w1(2)
+        load_member_s(3)
+        for g in range(D_PASSES):
+            second_product(0, g)
+        modulate(1)
+        skip_banks = [turn_skip(0, g) for g in range(D_PASSES)]
+        quantize_h(1, 0, 2)
+        add_skip(0, 0, skip_banks[0])
+        quantize_h(1, 2, 3)
+        add_skip(0, 1, skip_banks[1])
+        store_y(0)
+
+        last = N_TILES - 1
+        for i in range(TILES, N_TILES):
+            u = i + D_PASSES
+            has_unit = u < N_UNITS
+            first_product(i)
+            if i % TILES == 1 and i // TILES + 2 < E:
+                load_w1(i // TILES + 2)
+            if i % TILES == 1 and i // TILES + 3 < E:
+                load_member_s(i // TILES + 3)
+            round_y(i - 2)
+            if has_unit:
+                turn_s(u)
+                scale_s(u)
+                if u % D_PASSES == 0:
+                    join_skip(u // D_PASSES)
+            else:
+                skip_banks = [turn_skip(i - 1, g) for g in range(D_PASSES)]
+            modulate(i)
+            if has_unit:
+                finish_unit(u)
+                quantize_s(u)
+            else:
+                quantize_h(i, 0, 2)
+                quantize_h(i, 2, 3)
+            second_product(i - 1, 0)
+            if has_unit:
+                quantize_h(i, 0, 2)
+            second_product(i - 1, 1)
+            if i % TILES == 0 and i // TILES + 1 < E:
+                load_w2(i // TILES + 1)
+            if has_unit:
+                quantize_h(i, 2, 3)
+            if u + 1 < N_UNITS:
+                widen(u + 1)
+            if has_unit:
+                skip_banks = [turn_skip(i - 1, g) for g in range(D_PASSES)]
+            turn_y(i - 2)
+            add_skip(i - 1, 0, skip_banks[0])
+            quantize_y(i - 2)
+            add_skip(i - 1, 1, skip_banks[1])
+            store_y(i - 1)
+
+        store_scales(y_sc_early, 0, EARLY_TILES)
+        round_y(last - 1)
+        for g in range(D_PASSES):
+            second_product(last, g)
+        skip_banks = [turn_skip(last, g) for g in range(D_PASSES)]
+        turn_y(last - 1)
+        for g in range(D_PASSES):
+            add_skip(last, g, skip_banks[g])
+            store_y(last, g, g + 1)
+        for g in range(D_PASSES):
+            round_y(last, g, g + 1, copy=nc.vector.tensor_copy)
+        quantize_y(last - 1)
+        for g in range(D_PASSES):
+            turn_y(last, g, g + 1)
+            quantize_y(last, g, g + 1)
+        store_scales(y_sc_late, EARLY_TILES, TILES)

@@ -29,7 +29,8 @@ F_PASSES = F // K_PASS
 N_UNITS = E * D_PASSES
 QUADS = 4
 SCALE_SLOTS = 2
-EARLY_TILES = N_TILES - TILES
+LATE_TILES = 3
+EARLY_TILES = N_TILES - LATE_TILES
 
 
 def tile_ensemble_rollout_step_b12_kernel(
@@ -68,7 +69,7 @@ def tile_ensemble_rollout_step_b12_kernel(
         skip_scale = [keep.tile([P, D_PASSES, PACK], F32, name=f"skip_scale{e}") for e in range(E)]
         skip = keep.tile([P, D_PASSES, PACK], BF16)
         y_sc_early = keep.tile([P, D_PASSES, EARLY_TILES * P], U8, align_bytes=64)
-        y_sc_late = keep.tile([P, D_PASSES, TILES * P], U8, align_bytes=64)
+        y_sc_late = keep.tile([P, D_PASSES, LATE_TILES * P], U8, align_bytes=64)
 
         def by_word(row):
             return row.rearrange("(g p t) -> p g t", p=P, t=PACK)
@@ -108,6 +109,8 @@ def tile_ensemble_rollout_step_b12_kernel(
 
         def load_w2(e):
             load_weights(w2[e], w2_sc[e % SCALE_SLOTS], W2_words, W2_scales, e, F_PASSES)
+
+        def load_gain(e):
             nc.sync.dma_start(out=gain[e][:], in_=delta_gain[e].partition_broadcast(P))
 
         wide, v_bank, s_bf, s_codes, s_sc, skip_t = {}, {}, {}, {}, {}, {}
@@ -190,12 +193,13 @@ def tile_ensemble_rollout_step_b12_kernel(
             for t in range(PACK):
                 nc.tensor.transpose(bank[:, t * P : (t + 1) * P], plane_of(t), ident[:])
 
-        def modulate(i):
+        def modulate(i, first=0, last=F_PASSES):
             tt = i % TILES
-            h_bf[i] = work.tile([P, F_PASSES, K_PASS], BF16, name="h_bf", align_bytes=64)
-            h_codes[i] = work.tile([P, F_PASSES * P], U32, name="h_codes", align_bytes=64)
-            h_sc[i] = work.tile([P, F_PASSES * P], U8, name="h_sc", align_bytes=64)
-            for c in range(F_PASSES):
+            if first == 0:
+                h_bf[i] = work.tile([P, F_PASSES, K_PASS], BF16, name="h_bf", align_bytes=64)
+                h_codes[i] = work.tile([P, F_PASSES * P], U32, name="h_codes", align_bytes=64)
+                h_sc[i] = work.tile([P, F_PASSES * P], U8, name="h_sc", align_bytes=64)
+            for c in range(first, last):
                 b = next_bank()
                 bank = banks[b]
                 turn_planes(bank, lambda t: silu[i, c][:, t, :])
@@ -215,25 +219,30 @@ def tile_ensemble_rollout_step_b12_kernel(
                 in_=h_bf[i][:, first:last, :].rearrange("p c k -> p (c k)"),
             )
 
-        def second_product(i, g):
+        def second_pass(i, g, c, b):
             e = i // TILES
+            nc.tensor.matmul_mx(
+                out=banks[b][:],
+                lhsT=h_codes[i][:, c * P : (c + 1) * P].bitcast(FP8X4),
+                lhsT_scale=h_sc[i][:, c * P : (c + 1) * P],
+                rhs=w2[e][:, c, 2 * g * BANK : 2 * (g + 1) * BANK].bitcast(FP4X4),
+                rhs_scale=w2_sc[e % SCALE_SLOTS][:, c, g * BANK : (g + 1) * BANK],
+                start=(c == 0),
+                stop=(c == F_PASSES - 1),
+            )
+
+        def apply_gain(i, g, b):
             if g == 0:
                 y[i] = work.tile([P, D], F32, name="y", bufs=4)
             cols = slice(g * BANK, (g + 1) * BANK)
-            b = next_bank()
-            bank = banks[b]
-            for c in range(F_PASSES):
-                nc.tensor.matmul_mx(
-                    out=bank[:],
-                    lhsT=h_codes[i][:, c * P : (c + 1) * P].bitcast(FP8X4),
-                    lhsT_scale=h_sc[i][:, c * P : (c + 1) * P],
-                    rhs=w2[e][:, c, 2 * g * BANK : 2 * (g + 1) * BANK].bitcast(FP4X4),
-                    rhs_scale=w2_sc[e % SCALE_SLOTS][:, c, cols],
-                    start=(c == 0),
-                    stop=(c == F_PASSES - 1),
-                )
-            nc.vector.tensor_tensor(out=y[i][:, cols], in0=bank[:], in1=gain[e][:, cols], op=ALU.mult)
+            nc.vector.tensor_tensor(out=y[i][:, cols], in0=banks[b][:], in1=gain[i // TILES][:, cols], op=ALU.mult)
             free.append(b)
+
+        def second_product(i, g):
+            b = next_bank()
+            for c in range(F_PASSES):
+                second_pass(i, g, c, b)
+            apply_gain(i, g, b)
 
         def turn_skip(i, g):
             e, tt = divmod(i, TILES)
@@ -301,15 +310,17 @@ def tile_ensemble_rollout_step_b12_kernel(
         load_s(0)
         load_s(1)
         load_scale(0)
+        load_w1(0)
         nc.sync.dma_start(out=skip[:], in_=by_word(skip_gain))
         load_bias(0)
-        load_w1(0)
         nc.sync.dma_start(out=u_rows[:], in_=U.rearrange("(tt p) f -> p tt f", p=P))
         load_member_s(1)
         load_w2(0)
-        load_member_s(2)
         load_w1(1)
+        load_gain(0)
+        load_member_s(2)
         load_w2(1)
+        load_gain(1)
 
         def turn_u():
             for c in range(F_PASSES):
@@ -332,30 +343,29 @@ def tile_ensemble_rollout_step_b12_kernel(
         widen(1)
         turn_s(0)
         turn_s(1)
-        join_skip(0)
         for u in range(D_PASSES):
             scale_s(u, 0, P)
-            skip_term(u)
         for u in range(D_PASSES):
             quantize_s(u, 0, P)
-        first_product(0)
+        join_skip(0)
         scale_s(0, P, T)
+        finish_unit(0)
+        scale_s(1, P, T)
+        for u in range(D_PASSES):
+            quantize_s(u, P, T)
+        first_product(0)
         nc.vector.tensor_copy(
             out=u_sorted[:].rearrange("p tt (c h m) -> p (tt c) h m", h=2, m=P),
             in_=u_rows[:].bitcast(F32).rearrange("p tt (c m h) -> p (tt c) h m", h=2, m=P),
         )
-        scale_s(1, P, T)
-        free.extend(v_bank[u] for u in range(D_PASSES))
-        for u in range(D_PASSES):
-            quantize_s(u, P, T)
         widen(2, on_vector=True)
         widen(3, on_vector=True)
         join_skip(1)
         turn_u()
         modulate(0)
         first_product(1)
+        finish_unit(1)
         quantize_h(0, 0, 2)
-        widen(4, on_vector=True)
         quantize_h(0, 2, 3)
         for u in (2, 3):
             turn_s(u)
@@ -363,6 +373,7 @@ def tile_ensemble_rollout_step_b12_kernel(
         for u in (2, 3):
             quantize_s(u)
             finish_unit(u)
+        widen(4)
         load_w1(2)
         load_member_s(3)
         for g in range(D_PASSES):
@@ -392,7 +403,7 @@ def tile_ensemble_rollout_step_b12_kernel(
                     join_skip(u // D_PASSES)
             else:
                 skip_banks = [turn_skip(i - 1, g) for g in range(D_PASSES)]
-            modulate(i)
+            modulate(i, 0, 2 if has_unit else 3)
             if has_unit:
                 finish_unit(u)
                 quantize_s(u)
@@ -405,19 +416,23 @@ def tile_ensemble_rollout_step_b12_kernel(
             second_product(i - 1, 1)
             if i % TILES == 0 and i // TILES + 1 < E:
                 load_w2(i // TILES + 1)
+                load_gain(i // TILES + 1)
             if has_unit:
-                quantize_h(i, 2, 3)
+                modulate(i, 2, 3)
             if u + 1 < N_UNITS:
                 widen(u + 1)
             if has_unit:
                 skip_banks = [turn_skip(i - 1, g) for g in range(D_PASSES)]
             turn_y(i - 2)
             add_skip(i - 1, 0, skip_banks[0])
+            if has_unit:
+                quantize_h(i, 2, 3)
             quantize_y(i - 2)
+            if i - 2 == EARLY_TILES - 1:
+                store_scales(y_sc_early, 0, EARLY_TILES)
             add_skip(i - 1, 1, skip_banks[1])
             store_y(i - 1)
 
-        store_scales(y_sc_early, 0, EARLY_TILES)
         round_y(last - 1)
         for g in range(D_PASSES):
             second_product(last, g)
@@ -432,4 +447,4 @@ def tile_ensemble_rollout_step_b12_kernel(
         for g in range(D_PASSES):
             turn_y(last, g, g + 1)
             quantize_y(last, g, g + 1)
-        store_scales(y_sc_late, EARLY_TILES, TILES)
+        store_scales(y_sc_late, EARLY_TILES, LATE_TILES)

@@ -62,7 +62,7 @@ def tile_ensemble_rollout_step_b12_kernel(
         w2_sc = [keep.tile([P, F_PASSES, D], U8, name=f"w2_sc{s}", align_bytes=64) for s in range(SCALE_SLOTS)]
         gain = [keep.tile([P, D], BF16, name=f"gain{e}") for e in range(E)]
         u_rows = keep.tile([P, TILES, F], BF16)
-        u_t = keep.tile([P, F_PASSES, T, PACK], BF16)
+        u_t = keep.tile([P, F_PASSES - 1, T, PACK], BF16)
         u_sorted = keep.tile([P, TILES, F // 2], F32)
         scale = [keep.tile([P, D_PASSES, PACK], F32, name=f"scale{e}") for e in range(E)]
         bias = [keep.tile([P, D_PASSES, PACK], BF16, name=f"bias{e}") for e in range(E)]
@@ -95,6 +95,11 @@ def tile_ensemble_rollout_step_b12_kernel(
                 out=s_bytes[u][:], in_=S_bytes[e].rearrange("(tt p) (g k) -> g p tt k", p=P, k=K_PASS)[g]
             )
 
+        def load_s_tile(tt):
+            nc.sync.dma_start(
+                out=s_bytes[tt][:].rearrange("p g k -> p (g k)"), in_=S_bytes[0, tt * P : (tt + 1) * P, :]
+            )
+
         def load_weights(words_tile, scale_tile, words, scales, e, passes):
             rows = slice(e * passes, (e + 1) * passes)
             for q in range(QUADS):
@@ -114,6 +119,7 @@ def tile_ensemble_rollout_step_b12_kernel(
             nc.sync.dma_start(out=gain[e][:], in_=delta_gain[e].partition_broadcast(P))
 
         wide, v_bank, s_bf, s_codes, s_sc, skip_t = {}, {}, {}, {}, {}, {}
+        h_rows = {}
         silu, h_bf, h_codes, h_sc, y, y_bf, y_t = {}, {}, {}, {}, {}, {}, {}
 
         def widen(u, on_vector=False):
@@ -166,10 +172,13 @@ def tile_ensemble_rollout_step_b12_kernel(
                     bias=bias[e][:, g, t : t + 1], scale=skip_scale[e][:, g, t : t + 1],
                 )
 
-        def first_product(i):
+        def by_pairs(i, c):
+            return c == 0 or i == N_TILES - TILES
+
+        def first_product(i, chunks=(1, 2, 0)):
             e, tt = divmod(i, TILES)
             cols = slice(tt * P, (tt + 1) * P)
-            for c in range(F_PASSES):
+            for c in chunks:
                 b = next_bank()
                 bank = banks[b]
                 for g in range(D_PASSES):
@@ -183,33 +192,56 @@ def tile_ensemble_rollout_step_b12_kernel(
                         start=(g == 0),
                         stop=(g == D_PASSES - 1),
                     )
-                silu[i, c] = work.tile([P, PACK, P], F32, name="silu", bufs=6)
-                nc.scalar.activation(
-                    out=silu[i, c][:], in_=bank[:].rearrange("p (m t) -> p t m", t=PACK), func=ACT.Silu, bias=zero[:]
-                )
+                silu[i, c] = work.tile([P, BANK], F32, name="silu", bufs=6)
+                if by_pairs(i, c):
+                    src = bank[:].rearrange("p (m h b) -> p h m b", h=2, b=2)
+                    dst = silu[i, c][:].rearrange("p (h m b) -> p h m b", h=2, b=2)
+                else:
+                    src = bank[:].rearrange("p (m t) -> p t m", t=PACK)
+                    dst = silu[i, c][:].rearrange("p (t m) -> p t m", t=PACK)
+                nc.scalar.activation(out=dst, in_=src, func=ACT.Silu, bias=zero[:])
                 free.append(b)
 
         def turn_planes(bank, plane_of):
             for t in range(PACK):
                 nc.tensor.transpose(bank[:, t * P : (t + 1) * P], plane_of(t), ident[:])
 
-        def modulate(i, first=0, last=F_PASSES):
+        def new_h(i):
+            h_bf[i] = work.tile([P, F_PASSES, K_PASS], BF16, name="h_bf", align_bytes=64)
+            h_codes[i] = work.tile([P, F_PASSES * P], U32, name="h_codes", align_bytes=64)
+            h_sc[i] = work.tile([P, F_PASSES * P], U8, name="h_sc", align_bytes=64)
+
+        def turn_modulate(i, c):
             tt = i % TILES
-            if first == 0:
-                h_bf[i] = work.tile([P, F_PASSES, K_PASS], BF16, name="h_bf", align_bytes=64)
-                h_codes[i] = work.tile([P, F_PASSES * P], U32, name="h_codes", align_bytes=64)
-                h_sc[i] = work.tile([P, F_PASSES * P], U8, name="h_sc", align_bytes=64)
-            for c in range(first, last):
-                b = next_bank()
-                bank = banks[b]
-                turn_planes(bank, lambda t: silu[i, c][:, t, :])
-                nc.vector.tensor_tensor(
-                    out=h_bf[i][:, c, :].rearrange("p (m t) -> p m t", t=PACK),
-                    in0=bank[:].rearrange("p (t m) -> p m t", t=PACK),
-                    in1=u_t[:, c, tt * P : (tt + 1) * P, :],
-                    op=ALU.mult,
-                )
-                free.append(b)
+            b = next_bank()
+            turn_planes(banks[b], lambda t: silu[i, c][:, t * P : (t + 1) * P])
+            nc.vector.tensor_tensor(
+                out=h_bf[i][:, c, :].rearrange("p (m t) -> p m t", t=PACK),
+                in0=banks[b][:].rearrange("p (t m) -> p m t", t=PACK),
+                in1=u_t[:, c - 1, tt * P : (tt + 1) * P, :],
+                op=ALU.mult,
+            )
+            free.append(b)
+
+        def modulate_rows(i, c):
+            h_rows[i, c] = work.tile([P, K_PASS], BF16, name="h_rows", bufs=4)
+            nc.vector.tensor_tensor(
+                out=h_rows[i, c][:],
+                in0=silu[i, c][:],
+                in1=u_sorted[:, i % TILES, c * (K_PASS // 2) : (c + 1) * (K_PASS // 2)].bitcast(BF16),
+                op=ALU.mult,
+            )
+
+        def turn_rows(i, c):
+            b = next_bank()
+            words = h_rows[i, c][:].bitcast(F32)
+            for half in range(2):
+                nc.tensor.transpose(banks[b][:, half * P : (half + 1) * P], words[:, half * P : (half + 1) * P], ident[:])
+            nc.scalar.copy(
+                out=h_bf[i][:, c, :].bitcast(F32).rearrange("p (m h) -> p m h", h=2),
+                in_=banks[b][:, : 2 * P].rearrange("p (h m) -> p m h", h=2),
+            )
+            free.append(b)
 
         def quantize_h(i, first, last):
             cols = slice(first * P, last * P)
@@ -227,8 +259,8 @@ def tile_ensemble_rollout_step_b12_kernel(
                 lhsT_scale=h_sc[i][:, c * P : (c + 1) * P],
                 rhs=w2[e][:, c, 2 * g * BANK : 2 * (g + 1) * BANK].bitcast(FP4X4),
                 rhs_scale=w2_sc[e % SCALE_SLOTS][:, c, g * BANK : (g + 1) * BANK],
-                start=(c == 0),
-                stop=(c == F_PASSES - 1),
+                start=(c == 1),
+                stop=(c == 0),
             )
 
         def apply_gain(i, g, b):
@@ -240,7 +272,7 @@ def tile_ensemble_rollout_step_b12_kernel(
 
         def second_product(i, g):
             b = next_bank()
-            for c in range(F_PASSES):
+            for c in (1, 2, 0):
                 second_pass(i, g, c, b)
             apply_gain(i, g, b)
 
@@ -307,14 +339,17 @@ def tile_ensemble_rollout_step_b12_kernel(
         for s in range(SCALE_SLOTS):
             nc.vector.memset(w1_sc[s][:].bitcast(I32), 0)
             nc.vector.memset(w2_sc[s][:].bitcast(I32), 0)
-        load_s(0)
-        load_s(1)
+        load_s_tile(0)
+        load_s_tile(1)
         load_scale(0)
         load_w1(0)
         nc.sync.dma_start(out=skip[:], in_=by_word(skip_gain))
         load_bias(0)
+        load_s(2)
+        load_s(3)
         nc.sync.dma_start(out=u_rows[:], in_=U.rearrange("(tt p) f -> p tt f", p=P))
-        load_member_s(1)
+        load_scale(1)
+        load_bias(1)
         load_w2(0)
         load_w1(1)
         load_gain(0)
@@ -323,14 +358,14 @@ def tile_ensemble_rollout_step_b12_kernel(
         load_gain(1)
 
         def turn_u():
-            for c in range(F_PASSES):
+            for c in range(1, F_PASSES):
                 b = next_bank()
                 for half in range(2):
                     for tt in range(TILES):
                         col, word = half * T + tt * P, (2 * c + half) * P
                         nc.tensor.transpose(banks[b][:, col : col + P], u_sorted[:, tt, word : word + P], ident[:])
                 nc.scalar.copy(
-                    out=u_t[:, c].rearrange("p m t -> p (m t)").bitcast(F32).rearrange("p (m h) -> p m h", h=2),
+                    out=u_t[:, c - 1].rearrange("p m t -> p (m t)").bitcast(F32).rearrange("p (m h) -> p m h", h=2),
                     in_=banks[b][:].rearrange("p (h m) -> p m h", h=2),
                 )
                 free.append(b)
@@ -339,110 +374,159 @@ def tile_ensemble_rollout_step_b12_kernel(
             skip_term(u)
             free.append(v_bank[u])
 
+        def turn_first_member(tt):
+            words = wide[tt][:].bitcast(F32)
+            for g in range(D_PASSES):
+                for half in range(2):
+                    col, word = half * T + tt * P, g * (K_PASS // 2)
+                    nc.tensor.transpose(
+                        banks[v_bank[g]][:, col : col + P], words[:, word + half : word + K_PASS // 2 : 2], ident[:]
+                    )
+                scale_s(g, tt * P, (tt + 1) * P)
+                if tt == 1:
+                    if g == 0:
+                        join_skip(0)
+                    finish_unit(g)
+            for g in range(D_PASSES):
+                quantize_s(g, tt * P, (tt + 1) * P)
+
         widen(0, on_vector=True)
         widen(1)
-        turn_s(0)
-        turn_s(1)
-        for u in range(D_PASSES):
-            scale_s(u, 0, P)
-        for u in range(D_PASSES):
-            quantize_s(u, 0, P)
-        join_skip(0)
-        scale_s(0, P, T)
-        finish_unit(0)
-        scale_s(1, P, T)
-        for u in range(D_PASSES):
-            quantize_s(u, P, T)
+        for g in range(D_PASSES):
+            v_bank[g] = next_bank()
+        turn_first_member(0)
+        turn_first_member(1)
         first_product(0)
+        widen(2, on_vector=True)
+        widen(3, on_vector=True)
+        turn_s(2)
+        turn_s(3)
         nc.vector.tensor_copy(
             out=u_sorted[:].rearrange("p tt (c h m) -> p (tt c) h m", h=2, m=P),
             in_=u_rows[:].bitcast(F32).rearrange("p tt (c m h) -> p (tt c) h m", h=2, m=P),
         )
-        widen(2, on_vector=True)
-        widen(3, on_vector=True)
+        scale_s(2)
         join_skip(1)
+        first_product(1, (1, 2))
         turn_u()
-        modulate(0)
-        first_product(1)
-        finish_unit(1)
-        quantize_h(0, 0, 2)
-        quantize_h(0, 2, 3)
-        for u in (2, 3):
-            turn_s(u)
-            scale_s(u)
-        for u in (2, 3):
-            quantize_s(u)
-            finish_unit(u)
-        widen(4)
+        new_h(0)
+        modulate_rows(0, 0)
+        scale_s(3)
+        turn_modulate(0, 1)
+        turn_modulate(0, 2)
+        first_product(1, (0,))
+        turn_rows(0, 0)
+        finish_unit(2)
+        quantize_s(2)
+        quantize_h(0, 1, 3)
+        quantize_h(0, 0, 1)
+        quantize_s(3)
+        new_h(1)
+        modulate_rows(1, 0)
+        turn_modulate(1, 1)
+        turn_modulate(1, 2)
+        finish_unit(3)
         load_w1(2)
         load_member_s(3)
-        for g in range(D_PASSES):
-            second_product(0, g)
-        modulate(1)
         skip_banks = [turn_skip(0, g) for g in range(D_PASSES)]
-        quantize_h(1, 0, 2)
+        widen(4)
+        second_product(0, 0)
+        second_product(0, 1)
+        turn_rows(1, 0)
         add_skip(0, 0, skip_banks[0])
-        quantize_h(1, 2, 3)
+        quantize_h(1, 1, 3)
         add_skip(0, 1, skip_banks[1])
         store_y(0)
 
-        last = N_TILES - 1
-        for i in range(TILES, N_TILES):
+        for i in range(TILES, N_UNITS - D_PASSES):
             u = i + D_PASSES
-            has_unit = u < N_UNITS
             first_product(i)
             if i % TILES == 1 and i // TILES + 2 < E:
                 load_w1(i // TILES + 2)
             if i % TILES == 1 and i // TILES + 3 < E:
                 load_member_s(i // TILES + 3)
             round_y(i - 2)
-            if has_unit:
-                turn_s(u)
-                scale_s(u)
-                if u % D_PASSES == 0:
-                    join_skip(u // D_PASSES)
-            else:
-                skip_banks = [turn_skip(i - 1, g) for g in range(D_PASSES)]
-            modulate(i, 0, 2 if has_unit else 3)
-            if has_unit:
-                finish_unit(u)
-                quantize_s(u)
-            else:
-                quantize_h(i, 0, 2)
-                quantize_h(i, 2, 3)
+            quantize_h(i - 1, 0, 1)
+            new_h(i)
+            turn_s(u)
+            scale_s(u)
+            if u % D_PASSES == 0:
+                join_skip(u // D_PASSES)
+            modulate_rows(i, 0)
+            turn_modulate(i, 1)
+            turn_modulate(i, 2)
+            finish_unit(u)
+            quantize_s(u)
             second_product(i - 1, 0)
-            if has_unit:
-                quantize_h(i, 0, 2)
+            quantize_h(i, 1, 3)
             second_product(i - 1, 1)
             if i % TILES == 0 and i // TILES + 1 < E:
                 load_w2(i // TILES + 1)
                 load_gain(i // TILES + 1)
-            if has_unit:
-                modulate(i, 2, 3)
             if u + 1 < N_UNITS:
                 widen(u + 1)
-            if has_unit:
-                skip_banks = [turn_skip(i - 1, g) for g in range(D_PASSES)]
+            skip_banks = [turn_skip(i - 1, g) for g in range(D_PASSES)]
             turn_y(i - 2)
+            turn_rows(i, 0)
             add_skip(i - 1, 0, skip_banks[0])
-            if has_unit:
-                quantize_h(i, 2, 3)
             quantize_y(i - 2)
-            if i - 2 == EARLY_TILES - 1:
-                store_scales(y_sc_early, 0, EARLY_TILES)
             add_skip(i - 1, 1, skip_banks[1])
             store_y(i - 1)
 
-        round_y(last - 1)
+        last = N_TILES - 1
+        i = last - 1
+        first_product(i)
+        skip_banks = [turn_skip(i - 1, g) for g in range(D_PASSES)]
+        quantize_h(i - 1, 0, 1)
+        new_h(i)
+        for c in (1, 2, 0):
+            modulate_rows(i, c)
+        round_y(i - 2)
+        second_product(i - 1, 0)
+        second_product(i - 1, 1)
+        for c in (1, 2, 0):
+            turn_rows(i, c)
+        turn_y(i - 2)
+        add_skip(i - 1, 0, skip_banks[0])
+        quantize_h(i, 1, 3)
+        quantize_h(i, 0, 1)
+        add_skip(i - 1, 1, skip_banks[1])
+        quantize_y(i - 2)
+        store_scales(y_sc_early, 0, EARLY_TILES)
+        store_y(i - 1)
+
+        i = last
+        first_product(i, (0, 1, 2))
+        skip_banks = [turn_skip(i - 1, g) for g in range(D_PASSES)]
+        new_h(i)
+        modulate_rows(i, 0)
+        turn_modulate(i, 1)
+        turn_rows(i, 0)
+        turn_modulate(i, 2)
+        round_y(i - 2)
+        quantize_h(i, 0, 1)
+        quantize_h(i, 1, 3)
+        second_product(i - 1, 0)
+        second_product(i - 1, 1)
+        out_banks = [next_bank() for g in range(D_PASSES)]
         for g in range(D_PASSES):
-            second_product(last, g)
+            for c in (1, 2, 0):
+                second_pass(last, g, c, out_banks[g])
+        add_skip(i - 1, 0, skip_banks[0])
+        add_skip(i - 1, 1, skip_banks[1])
+        store_y(i - 1)
         skip_banks = [turn_skip(last, g) for g in range(D_PASSES)]
+        round_y(last - 1)
+        turn_y(i - 2)
+        for g in range(D_PASSES):
+            apply_gain(last, g, out_banks[g])
         turn_y(last - 1)
         for g in range(D_PASSES):
             add_skip(last, g, skip_banks[g])
             store_y(last, g, g + 1)
         for g in range(D_PASSES):
             round_y(last, g, g + 1, copy=nc.vector.tensor_copy)
+        quantize_y(last - 2)
         quantize_y(last - 1)
         for g in range(D_PASSES):
             turn_y(last, g, g + 1)

@@ -232,6 +232,15 @@ def tile_ensemble_rollout_step_b12_kernel(
                 op=ALU.mult,
             )
 
+        def modulate_rows_aside(i):
+            h_rows[i, 0] = h_bf[i - 1][:, 0, :]
+            nc.gpsimd.tensor_tensor(
+                out=h_rows[i, 0],
+                in0=silu[i, 0][:],
+                in1=u_sorted[:, i % TILES, : K_PASS // 2].bitcast(BF16),
+                op=ALU.mult,
+            )
+
         def turn_rows(i, c):
             b = next_bank()
             words = h_rows[i, c][:].bitcast(F32)
@@ -292,19 +301,21 @@ def tile_ensemble_rollout_step_b12_kernel(
             cols = slice(first * K_PASS, last * K_PASS)
             nc.sync.dma_start(out=out_0[e, tt * P : (tt + 1) * P, cols], in_=y[i][:, cols])
 
-        def round_y(i, first=0, last=D_PASSES, copy=nc.scalar.copy):
-            y_bf[i, first] = work.tile([P, (last - first) * K_PASS], BF16, name="y_bf", bufs=3)
+        def round_y(i, g, copy):
+            y_bf[i, g] = work.tile([P, K_PASS], BF16, name="y_bf", bufs=6)
             copy(
-                out=y_bf[i, first][:].rearrange("p (g h m b) -> p g h m b", m=P, h=2, b=2),
-                in_=y[i][:, first * K_PASS : last * K_PASS].rearrange("p (g m h b) -> p g h m b", m=P, h=2, b=2),
+                out=y_bf[i, g][:].rearrange("p (h m b) -> p h m b", h=2, b=2),
+                in_=y[i][:, g * K_PASS : (g + 1) * K_PASS].rearrange("p (m h b) -> p h m b", h=2, b=2),
             )
 
         def turn_y(i, first=0, last=D_PASSES):
             b = next_bank()
             bank = banks[b]
-            words = y_bf[i, first][:].bitcast(F32)
-            for j in range(2 * (last - first)):
-                nc.tensor.transpose(bank[:, j * P : (j + 1) * P], words[:, j * P : (j + 1) * P], ident[:])
+            for g in range(first, last):
+                words = y_bf[i, g][:].bitcast(F32)
+                for half in range(2):
+                    col = (2 * (g - first) + half) * P
+                    nc.tensor.transpose(bank[:, col : col + P], words[:, half * P : (half + 1) * P], ident[:])
             y_t[i, first] = work.tile([P, (last - first) * K_PASS], BF16, name="y_t", bufs=3, align_bytes=64)
             nc.scalar.copy(
                 out=y_t[i, first][:].bitcast(F32).rearrange("p (g m h) -> p g m h", m=P, h=2),
@@ -312,9 +323,9 @@ def tile_ensemble_rollout_step_b12_kernel(
             )
             free.append(b)
 
-        def store_scales(plane, first, count):
+        def store_scales(plane, first, count, queues):
             for q in range(QUADS):
-                nc.sync.dma_start(
+                queues[q % len(queues)].dma_start(
                     out=out_2[:, 4 * q : 4 * q + 4, first * P : (first + count) * P].rearrange("g r m -> r g m").bitcast(I32),
                     in_=plane[32 * q : 32 * q + 4].bitcast(I32),
                 )
@@ -436,6 +447,7 @@ def tile_ensemble_rollout_step_b12_kernel(
         add_skip(0, 0, skip_banks[0])
         quantize_h(1, 1, 3)
         add_skip(0, 1, skip_banks[1])
+        round_y(0, 0, nc.vector.tensor_copy)
         store_y(0)
 
         for i in range(TILES, N_UNITS - D_PASSES):
@@ -445,14 +457,14 @@ def tile_ensemble_rollout_step_b12_kernel(
                 load_w1(i // TILES + 2)
             if i % TILES == 1 and i // TILES + 3 < E:
                 load_member_s(i // TILES + 3)
-            round_y(i - 2)
+            round_y(i - 2, 1, nc.scalar.copy)
             quantize_h(i - 1, 0, 1)
             new_h(i)
             turn_s(u)
             scale_s(u)
             if u % D_PASSES == 0:
                 join_skip(u // D_PASSES)
-            modulate_rows(i, 0)
+            modulate_rows_aside(i)
             turn_modulate(i, 1)
             turn_modulate(i, 2)
             finish_unit(u)
@@ -471,6 +483,8 @@ def tile_ensemble_rollout_step_b12_kernel(
             add_skip(i - 1, 0, skip_banks[0])
             quantize_y(i - 2)
             add_skip(i - 1, 1, skip_banks[1])
+            if u + 1 < N_UNITS:
+                round_y(i - 1, 0, nc.vector.tensor_copy)
             store_y(i - 1)
 
         last = N_TILES - 1
@@ -481,7 +495,8 @@ def tile_ensemble_rollout_step_b12_kernel(
         new_h(i)
         for c in (1, 2, 0):
             modulate_rows(i, c)
-        round_y(i - 2)
+        for g in range(D_PASSES):
+            round_y(i - 2, g, nc.scalar.copy)
         second_product(i - 1, 0)
         second_product(i - 1, 1)
         for c in (1, 2, 0):
@@ -492,7 +507,7 @@ def tile_ensemble_rollout_step_b12_kernel(
         quantize_h(i, 0, 1)
         add_skip(i - 1, 1, skip_banks[1])
         quantize_y(i - 2)
-        store_scales(y_sc_early, 0, EARLY_TILES)
+        store_scales(y_sc_early, 0, EARLY_TILES, [nc.sync])
         store_y(i - 1)
 
         i = last
@@ -503,7 +518,8 @@ def tile_ensemble_rollout_step_b12_kernel(
         turn_modulate(i, 1)
         turn_rows(i, 0)
         turn_modulate(i, 2)
-        round_y(i - 2)
+        for g in range(D_PASSES):
+            round_y(i - 2, g, nc.scalar.copy)
         quantize_h(i, 0, 1)
         quantize_h(i, 1, 3)
         second_product(i - 1, 0)
@@ -516,7 +532,8 @@ def tile_ensemble_rollout_step_b12_kernel(
         add_skip(i - 1, 1, skip_banks[1])
         store_y(i - 1)
         skip_banks = [turn_skip(last, g) for g in range(D_PASSES)]
-        round_y(last - 1)
+        for g in range(D_PASSES):
+            round_y(last - 1, g, nc.scalar.copy)
         turn_y(i - 2)
         for g in range(D_PASSES):
             apply_gain(last, g, out_banks[g])
@@ -525,10 +542,10 @@ def tile_ensemble_rollout_step_b12_kernel(
             add_skip(last, g, skip_banks[g])
             store_y(last, g, g + 1)
         for g in range(D_PASSES):
-            round_y(last, g, g + 1, copy=nc.vector.tensor_copy)
+            round_y(last, g, nc.vector.tensor_copy)
         quantize_y(last - 2)
         quantize_y(last - 1)
         for g in range(D_PASSES):
             turn_y(last, g, g + 1)
             quantize_y(last, g, g + 1)
-        store_scales(y_sc_late, EARLY_TILES, LATE_TILES)
+        store_scales(y_sc_late, EARLY_TILES, LATE_TILES, [nc.scalar, nc.sync])

from contextlib import ExitStack

import concourse.mybir as mybir
from concourse.masks import make_identity

E, T, D, F = 5, 256, 1024, 1536
FLOPS = 2 * E * T * D * F * 2

F32 = mybir.dt.float32
BF16 = mybir.dt.bfloat16
I32 = mybir.dt.int32
U32 = mybir.dt.uint32
U8 = mybir.dt.uint8
FP8 = mybir.dt.float8_e4m3fn
FP8X4 = mybir.dt.float8_e4m3fn_x4
FP4X4 = mybir.dt.float4_e2m1fn_x4
ACT = mybir.ActivationFunctionType
ALU = mybir.AluOpType

P = 128
PACK = 4
K_PASS = P * PACK
BANK = 512
N_BANKS = 8
TILES = T // P
N_TILES = E * TILES
D_PASSES = D // K_PASS
F_PASSES = F // K_PASS
N_UNITS = E * D_PASSES
QUADS = 4
SCALE_SLOTS = 2
LATE_TILES = 3
EARLY_TILES = N_TILES - LATE_TILES


def tile_ensemble_rollout_step_b12_kernel(
    tc, S_bytes, S_scale, U, W1_words, W1_scales, W2_words, W2_scales, skip_gain, delta_gain, delta_bias,
    out_0, out_1, out_2,
):
    nc = tc.nc
    with ExitStack() as ctx:
        keep = ctx.enter_context(tc.tile_pool(name="keep", bufs=1))
        work = ctx.enter_context(tc.tile_pool(name="work", bufs=2))
        psum = ctx.enter_context(tc.psum_pool(name="psum", bufs=1))
        ctx.enter_context(tc.manual_schedule())

        banks = [psum.tile([P, BANK], F32, name=f"bank{b}") for b in range(N_BANKS)]
        free = list(range(N_BANKS))

        def next_bank():
            b = free[0]
            free.remove(b)
            return b

        ident = keep.tile([P, P], F32)
        zero_in = keep.tile([P, 1], F32)
        zero = keep.tile([P, 1], F32)
        s_bytes = [keep.tile([P, TILES, K_PASS], U8, name=f"s_bytes{u}") for u in range(N_UNITS)]
        w1 = [keep.tile([P, D_PASSES, 2 * F], U8, name=f"w1_{e}", align_bytes=64) for e in range(E)]
        w2 = [keep.tile([P, F_PASSES, 2 * D], U8, name=f"w2_{e}", align_bytes=64) for e in range(E)]
        w1_sc = [keep.tile([P, D_PASSES, F], U8, name=f"w1_sc{s}", align_bytes=64) for s in range(SCALE_SLOTS)]
        w2_sc = [keep.tile([P, F_PASSES, D], U8, name=f"w2_sc{s}", align_bytes=64) for s in range(SCALE_SLOTS)]
        gain = [keep.tile([P, D], BF16, name=f"gain{e}") for e in range(E)]
        u_rows = keep.tile([P, TILES, F], BF16)
        u_t = keep.tile([P, F_PASSES - 1, T, PACK], BF16)
        u_sorted = keep.tile([P, TILES, F // 2], F32)
        scale = [keep.tile([P, D_PASSES, PACK], F32, name=f"scale{e}") for e in range(E)]
        bias = [keep.tile([P, D_PASSES, PACK], BF16, name=f"bias{e}") for e in range(E)]
        skip_scale = [keep.tile([P, D_PASSES, PACK], F32, name=f"skip_scale{e}") for e in range(E)]
        skip = keep.tile([P, D_PASSES, PACK], BF16)
        y_sc_early = keep.tile([P, D_PASSES, EARLY_TILES * P], U8, align_bytes=64)
        y_sc_late = keep.tile([P, D_PASSES, LATE_TILES * P], U8, align_bytes=64)

        def by_word(row):
            return row.rearrange("(g p t) -> p g t", p=P, t=PACK)

        def load_scale(e):
            nc.sync.dma_start(out=scale[e][:], in_=by_word(S_scale[e, 0]))

        def load_bias(e):
            nc.sync.dma_start(out=bias[e][:], in_=by_word(delta_bias[e]))

        def load_member_s(e):
            for g in range(D_PASSES):
                load_s(e * D_PASSES + g)
            load_scale(e)
            load_bias(e)

        def join_skip(e):
            nc.vector.tensor_tensor(out=skip_scale[e][:], in0=scale[e][:], in1=skip[:], op=ALU.mult)

        def load_s(u):
            e, g = divmod(u, D_PASSES)
            nc.sync.dma_start(
                out=s_bytes[u][:], in_=S_bytes[e].rearrange("(tt p) (g k) -> g p tt k", p=P, k=K_PASS)[g]
            )

        def load_s_tile(tt):
            nc.sync.dma_start(
                out=s_bytes[tt][:].rearrange("p g k -> p (g k)"), in_=S_bytes[0, tt * P : (tt + 1) * P, :]
            )

        def load_weights(words_tile, scale_tile, words, scales, e, passes):
            rows = slice(e * passes, (e + 1) * passes)
            for q in range(QUADS):
                nc.sync.dma_start(
                    out=scale_tile[32 * q : 32 * q + 4].bitcast(I32),
                    in_=scales[rows, 4 * q : 4 * q + 4, :].rearrange("g r n -> r g n").bitcast(I32),
                )
            nc.sync.dma_start(out=words_tile[:].bitcast(I32), in_=words[rows].rearrange("g p n -> p g n").bitcast(I32))

        def load_w1(e):
            load_weights(w1[e], w1_sc[e % SCALE_SLOTS], W1_words, W1_scales, e, D_PASSES)

        def load_w2(e):
            load_weights(w2[e], w2_sc[e % SCALE_SLOTS], W2_words, W2_scales, e, F_PASSES)

        def load_gain(e):
            nc.sync.dma_start(out=gain[e][:], in_=delta_gain[e].partition_broadcast(P))

        wide, v_bank, s_bf, s_codes, s_sc, skip_t = {}, {}, {}, {}, {}, {}
        h_rows = {}
        silu, h_bf, h_codes, h_sc, y, y_bf, y_t = {}, {}, {}, {}, {}, {}, {}

        def widen(u, on_vector=False):
            wide[u] = work.tile([P, TILES * K_PASS], BF16, name="wide", bufs=3)
            codes = s_bytes[u][:].rearrange("p tt k -> p (tt k)").bitcast(FP8)
            if on_vector:
                nc.vector.tensor_copy(out=wide[u][:], in_=codes)
            else:
                nc.scalar.copy(out=wide[u][:], in_=codes)

        def turn_pairs(bank, words_of):
            for half in range(2):
                for tt in range(TILES):
                    col = half * T + tt * P
                    nc.tensor.transpose(bank[:, col : col + P], words_of(tt)[:, half : K_PASS // 2 : 2], ident[:])

        def turn_s(u):
            v_bank[u] = next_bank()
            words = wide[u][:].bitcast(F32)
            turn_pairs(banks[v_bank[u]], lambda tt: words[:, tt * (K_PASS // 2) : (tt + 1) * (K_PASS // 2)])

        def scale_s(u, first=0, last=T):
            e, g = divmod(u, D_PASSES)
            if first == 0:
                s_bf[u] = work.tile([P, T * PACK], BF16, name="s_bf", bufs=2, align_bytes=64)
            nc.vector.tensor_tensor(
                out=s_bf[u][:].rearrange("p (m h b) -> p m h b", h=2, b=2)[:, first:last],
                in0=banks[v_bank[u]][:].bitcast(BF16).rearrange("p (h m b) -> p m h b", h=2, b=2)[:, first:last],
                in1=scale[e][:, g, :].rearrange("p (h b) -> p h b", b=2).unsqueeze(1).to_broadcast([P, last - first, 2, 2]),
                op=ALU.mult,
            )

        def quantize_s(u, first=0, last=T):
            if first == 0:
                s_codes[u] = work.tile([P, T], U32, name="s_codes", bufs=4, align_bytes=64)
                s_sc[u] = work.tile([P, T], U8, name="s_sc", bufs=4, align_bytes=64)
            nc.vector.quantize_mx(
                out=s_codes[u][:, first:last].bitcast(FP8X4),
                scales=s_sc[u][:, first:last],
                in_=s_bf[u][:, first * PACK : last * PACK],
            )

        def skip_term(u):
            e, g = divmod(u, D_PASSES)
            skip_t[u] = work.tile([P, PACK, T], F32, name="skip_t", bufs=6)
            values = banks[v_bank[u]][:].bitcast(BF16).rearrange("p (h m b) -> p h b m", h=2, b=2)
            for t in range(PACK):
                nc.scalar.activation(
                    out=skip_t[u][:, t, :], in_=values[:, t // 2, t % 2, :], func=ACT.Identity,
                    bias=bias[e][:, g, t : t + 1], scale=skip_scale[e][:, g, t : t + 1],
                )

        def by_pairs(i, c):
            return c == 0 or i == N_TILES - TILES

        def first_product(i, chunks=(1, 2, 0)):
            e, tt = divmod(i, TILES)
            cols = slice(tt * P, (tt + 1) * P)
            for c in chunks:
                b = next_bank()
                bank = banks[b]
                for g in range(D_PASSES):
                    u = e * D_PASSES + g
                    nc.tensor.matmul_mx(
                        out=bank[:],
                        lhsT=s_codes[u][:, cols].bitcast(FP8X4),
                        lhsT_scale=s_sc[u][:, cols],
                        rhs=w1[e][:, g, 2 * c * BANK : 2 * (c + 1) * BANK].bitcast(FP4X4),
                        rhs_scale=w1_sc[e % SCALE_SLOTS][:, g, c * BANK : (c + 1) * BANK],
                        start=(g == 0),
                        stop=(g == D_PASSES - 1),
                    )
                silu[i, c] = work.tile([P, BANK], F32, name="silu", bufs=6)
                if by_pairs(i, c):
                    src = bank[:].rearrange("p (m h b) -> p h m b", h=2, b=2)
                    dst = silu[i, c][:].rearrange("p (h m b) -> p h m b", h=2, b=2)
                else:
                    src = bank[:].rearrange("p (m t) -> p t m", t=PACK)
                    dst = silu[i, c][:].rearrange("p (t m) -> p t m", t=PACK)
                nc.scalar.activation(out=dst, in_=src, func=ACT.Silu, bias=zero[:])
                free.append(b)

        def turn_planes(bank, plane_of):
            for t in range(PACK):
                nc.tensor.transpose(bank[:, t * P : (t + 1) * P], plane_of(t), ident[:])

        def new_h(i):
            h_bf[i] = work.tile([P, F_PASSES, K_PASS], BF16, name="h_bf", align_bytes=64)
            h_codes[i] = work.tile([P, F_PASSES * P], U32, name="h_codes", align_bytes=64)
            h_sc[i] = work.tile([P, F_PASSES * P], U8, name="h_sc", align_bytes=64)

        def turn_modulate(i, c):
            tt = i % TILES
            b = next_bank()
            turn_planes(banks[b], lambda t: silu[i, c][:, t * P : (t + 1) * P])
            nc.vector.tensor_tensor(
                out=h_bf[i][:, c, :].rearrange("p (m t) -> p m t", t=PACK),
                in0=banks[b][:].rearrange("p (t m) -> p m t", t=PACK),
                in1=u_t[:, c - 1, tt * P : (tt + 1) * P, :],
                op=ALU.mult,
            )
            free.append(b)

        def modulate_rows(i, c):
            h_rows[i, c] = work.tile([P, K_PASS], BF16, name="h_rows", bufs=4)
            nc.vector.tensor_tensor(
                out=h_rows[i, c][:],
                in0=silu[i, c][:],
                in1=u_sorted[:, i % TILES, c * (K_PASS // 2) : (c + 1) * (K_PASS // 2)].bitcast(BF16),
                op=ALU.mult,
            )

        def modulate_rows_aside(i):
            h_rows[i, 0] = h_bf[i - 1][:, 0, :]
            nc.gpsimd.tensor_tensor(
                out=h_rows[i, 0],
                in0=silu[i, 0][:],
                in1=u_sorted[:, i % TILES, : K_PASS // 2].bitcast(BF16),
                op=ALU.mult,
            )

        def turn_rows(i, c):
            b = next_bank()
            words = h_rows[i, c][:].bitcast(F32)
            for half in range(2):
                nc.tensor.transpose(banks[b][:, half * P : (half + 1) * P], words[:, half * P : (half + 1) * P], ident[:])
            nc.scalar.copy(
                out=h_bf[i][:, c, :].bitcast(F32).rearrange("p (m h) -> p m h", h=2),
                in_=banks[b][:, : 2 * P].rearrange("p (h m) -> p m h", h=2),
            )
            free.append(b)

        def quantize_h(i, first, last):
            cols = slice(first * P, last * P)
            nc.vector.quantize_mx(
                out=h_codes[i][:, cols].bitcast(FP8X4),
                scales=h_sc[i][:, cols],
                in_=h_bf[i][:, first:last, :].rearrange("p c k -> p (c k)"),
            )

        def second_pass(i, g, c, b):
            e = i // TILES
            nc.tensor.matmul_mx(
                out=banks[b][:],
                lhsT=h_codes[i][:, c * P : (c + 1) * P].bitcast(FP8X4),
                lhsT_scale=h_sc[i][:, c * P : (c + 1) * P],
                rhs=w2[e][:, c, 2 * g * BANK : 2 * (g + 1) * BANK].bitcast(FP4X4),
                rhs_scale=w2_sc[e % SCALE_SLOTS][:, c, g * BANK : (g + 1) * BANK],
                start=(c == 1),
                stop=(c == 0),
            )

        def apply_gain(i, g, b):
            if g == 0:
                y[i] = work.tile([P, D], F32, name="y", bufs=4)
            cols = slice(g * BANK, (g + 1) * BANK)
            nc.vector.tensor_tensor(out=y[i][:, cols], in0=banks[b][:], in1=gain[i // TILES][:, cols], op=ALU.mult)
            free.append(b)

        def second_product(i, g):
            b = next_bank()
            for c in (1, 2, 0):
                second_pass(i, g, c, b)
            apply_gain(i, g, b)

        def turn_skip(i, g):
            e, tt = divmod(i, TILES)
            b = next_bank()
            turn_planes(banks[b], lambda t: skip_t[e * D_PASSES + g][:, t, tt * P : (tt + 1) * P])
            return b

        def add_skip(i, g, b):
            part = y[i][:, g * BANK : (g + 1) * BANK].rearrange("p (m t) -> p m t", t=PACK)
            nc.vector.tensor_tensor(out=part, in0=banks[b][:].rearrange("p (t m) -> p m t", t=PACK), in1=part, op=ALU.add)
            free.append(b)

        def store_y(i, first=0, last=D_PASSES):
            e, tt = divmod(i, TILES)
            cols = slice(first * K_PASS, last * K_PASS)
            nc.sync.dma_start(out=out_0[e, tt * P : (tt + 1) * P, cols], in_=y[i][:, cols])

        def round_y(i, g, copy):
            y_bf[i, g] = work.tile([P, K_PASS], BF16, name="y_bf", bufs=6)
            copy(
                out=y_bf[i, g][:].rearrange("p (h m b) -> p h m b", h=2, b=2),
                in_=y[i][:, g * K_PASS : (g + 1) * K_PASS].rearrange("p (m h b) -> p h m b", h=2, b=2),
            )

        def turn_y(i, first=0, last=D_PASSES):
            b = next_bank()
            bank = banks[b]
            for g in range(first, last):
                words = y_bf[i, g][:].bitcast(F32)
                for half in range(2):
                    col = (2 * (g - first) + half) * P
                    nc.tensor.transpose(bank[:, col : col + P], words[:, half * P : (half + 1) * P], ident[:])
            y_t[i, first] = work.tile([P, (last - first) * K_PASS], BF16, name="y_t", bufs=3, align_bytes=64)
            nc.scalar.copy(
                out=y_t[i, first][:].bitcast(F32).rearrange("p (g m h) -> p g m h", m=P, h=2),
                in_=bank[:, : 2 * (last - first) * P].rearrange("p (g h m) -> p g m h", m=P, h=2),
            )
            free.append(b)

        def store_scales(plane, first, count, queues):
            for q in range(QUADS):
                queues[q % len(queues)].dma_start(
                    out=out_2[:, 4 * q : 4 * q + 4, first * P : (first + count) * P].rearrange("g r m -> r g m").bitcast(I32),
                    in_=plane[32 * q : 32 * q + 4].bitcast(I32),
                )

        def quantize_y(i, first=0, last=D_PASSES):
            y_codes = work.tile([P, last - first, P], U32, name="y_codes", bufs=4, align_bytes=64)
            plane, at = (y_sc_early, i) if i < EARLY_TILES else (y_sc_late, i - EARLY_TILES)
            for g in range(first, last):
                nc.vector.quantize_mx(
                    out=y_codes[:, g - first, :].bitcast(FP8X4),
                    scales=plane[:, g, at * P : (at + 1) * P],
                    in_=y_t[i, first][:, (g - first) * K_PASS : (g - first + 1) * K_PASS],
                )
            nc.sync.dma_start(
                out=out_1[first:last, :, i * P : (i + 1) * P, :].rearrange("g p m t -> p g (m t)").bitcast(I32),
                in_=y_codes[:].bitcast(I32),
            )

        make_identity(nc, ident[:])
        nc.vector.memset(zero_in[:], 0.0)
        nc.scalar.activation(out=zero[:], in_=zero_in[:], func=ACT.Silu)
        for s in range(SCALE_SLOTS):
            nc.vector.memset(w1_sc[s][:].bitcast(I32), 0)
            nc.vector.memset(w2_sc[s][:].bitcast(I32), 0)
        load_s_tile(0)
        load_s_tile(1)
        load_scale(0)
        load_w1(0)
        nc.sync.dma_start(out=skip[:], in_=by_word(skip_gain))
        load_bias(0)
        load_s(2)
        load_s(3)
        nc.sync.dma_start(out=u_rows[:], in_=U.rearrange("(tt p) f -> p tt f", p=P))
        load_scale(1)
        load_bias(1)
        load_w2(0)
        load_w1(1)
        load_gain(0)
        load_member_s(2)
        load_w2(1)
        load_gain(1)

        def turn_u():
            for c in range(1, F_PASSES):
                b = next_bank()
                for half in range(2):
                    for tt in range(TILES):
                        col, word = half * T + tt * P, (2 * c + half) * P
                        nc.tensor.transpose(banks[b][:, col : col + P], u_sorted[:, tt, word : word + P], ident[:])
                nc.scalar.copy(
                    out=u_t[:, c - 1].rearrange("p m t -> p (m t)").bitcast(F32).rearrange("p (m h) -> p m h", h=2),
                    in_=banks[b][:].rearrange("p (h m) -> p m h", h=2),
                )
                free.append(b)

        def finish_unit(u):
            skip_term(u)
            free.append(v_bank[u])

        def turn_first_member(tt):
            words = wide[tt][:].bitcast(F32)
            for g in range(D_PASSES):
                for half in range(2):
                    col, word = half * T + tt * P, g * (K_PASS // 2)
                    nc.tensor.transpose(
                        banks[v_bank[g]][:, col : col + P], words[:, word + half : word + K_PASS // 2 : 2], ident[:]
                    )
                scale_s(g, tt * P, (tt + 1) * P)
                if tt == 1:
                    if g == 0:
                        join_skip(0)
                    finish_unit(g)
            for g in range(D_PASSES):
                quantize_s(g, tt * P, (tt + 1) * P)

        widen(0, on_vector=True)
        widen(1)
        for g in range(D_PASSES):
            v_bank[g] = next_bank()
        turn_first_member(0)
        turn_first_member(1)
        first_product(0)
        widen(2, on_vector=True)
        widen(3, on_vector=True)
        turn_s(2)
        turn_s(3)
        nc.vector.tensor_copy(
            out=u_sorted[:].rearrange("p tt (c h m) -> p (tt c) h m", h=2, m=P),
            in_=u_rows[:].bitcast(F32).rearrange("p tt (c m h) -> p (tt c) h m", h=2, m=P),
        )
        scale_s(2)
        join_skip(1)
        first_product(1, (1, 2))
        turn_u()
        new_h(0)
        modulate_rows(0, 0)
        scale_s(3)
        turn_modulate(0, 1)
        turn_modulate(0, 2)
        first_product(1, (0,))
        turn_rows(0, 0)
        finish_unit(2)
        quantize_s(2)
        quantize_h(0, 1, 3)
        quantize_h(0, 0, 1)
        quantize_s(3)
        new_h(1)
        modulate_rows(1, 0)
        turn_modulate(1, 1)
        turn_modulate(1, 2)
        finish_unit(3)
        load_w1(2)
        load_member_s(3)
        skip_banks = [turn_skip(0, g) for g in range(D_PASSES)]
        widen(4)
        second_product(0, 0)
        second_product(0, 1)
        turn_rows(1, 0)
        add_skip(0, 0, skip_banks[0])
        quantize_h(1, 1, 3)
        add_skip(0, 1, skip_banks[1])
        round_y(0, 0, nc.vector.tensor_copy)
        store_y(0)

        for i in range(TILES, N_UNITS - D_PASSES):
            u = i + D_PASSES
            first_product(i)
            if i % TILES == 1 and i // TILES + 2 < E:
                load_w1(i // TILES + 2)
            if i % TILES == 1 and i // TILES + 3 < E:
                load_member_s(i // TILES + 3)
            round_y(i - 2, 1, nc.scalar.copy)
            quantize_h(i - 1, 0, 1)
            new_h(i)
            turn_s(u)
            scale_s(u)
            if u % D_PASSES == 0:
                join_skip(u // D_PASSES)
            modulate_rows_aside(i)
            turn_modulate(i, 1)
            turn_modulate(i, 2)
            finish_unit(u)
            quantize_s(u)
            second_product(i - 1, 0)
            quantize_h(i, 1, 3)
            second_product(i - 1, 1)
            if i % TILES == 0 and i // TILES + 1 < E:
                load_w2(i // TILES + 1)
                load_gain(i // TILES + 1)
            if u + 1 < N_UNITS:
                widen(u + 1)
            skip_banks = [turn_skip(i - 1, g) for g in range(D_PASSES)]
            turn_y(i - 2)
            turn_rows(i, 0)
            add_skip(i - 1, 0, skip_banks[0])
            quantize_y(i - 2)
            add_skip(i - 1, 1, skip_banks[1])
            if u + 1 < N_UNITS:
                round_y(i - 1, 0, nc.vector.tensor_copy)
            store_y(i - 1)

        last = N_TILES - 1
        i = last - 1
        first_product(i)
        skip_banks = [turn_skip(i - 1, g) for g in range(D_PASSES)]
        quantize_h(i - 1, 0, 1)
        new_h(i)
        for c in (1, 2, 0):
            modulate_rows(i, c)
        for g in range(D_PASSES):
            round_y(i - 2, g, nc.scalar.copy)
        second_product(i - 1, 0)
        second_product(i - 1, 1)
        for c in (1, 2, 0):
            turn_rows(i, c)
        turn_y(i - 2)
        add_skip(i - 1, 0, skip_banks[0])
        quantize_h(i, 1, 3)
        quantize_h(i, 0, 1)
        add_skip(i - 1, 1, skip_banks[1])
        quantize_y(i - 2)
        store_scales(y_sc_early, 0, EARLY_TILES, [nc.sync])
        store_y(i - 1)

        i = last
        first_product(i, (0, 1, 2))
        skip_banks = [turn_skip(i - 1, g) for g in range(D_PASSES)]
        new_h(i)
        modulate_rows(i, 0)
        turn_modulate(i, 1)
        turn_rows(i, 0)
        turn_modulate(i, 2)
        for g in range(D_PASSES):
            round_y(i - 2, g, nc.scalar.copy)
        quantize_h(i, 0, 1)
        quantize_h(i, 1, 3)
        second_product(i - 1, 0)
        second_product(i - 1, 1)
        out_banks = [next_bank() for g in range(D_PASSES)]
        for g in range(D_PASSES):
            for c in (1, 2, 0):
                second_pass(last, g, c, out_banks[g])
        add_skip(i - 1, 0, skip_banks[0])
        add_skip(i - 1, 1, skip_banks[1])
        store_y(i - 1)
        skip_banks = [turn_skip(last, g) for g in range(D_PASSES)]
        for g in range(D_PASSES):
            round_y(last - 1, g, nc.scalar.copy)
        turn_y(i - 2)
        for g in range(D_PASSES):
            apply_gain(last, g, out_banks[g])
        turn_y(last - 1)
        for g in range(D_PASSES):
            add_skip(last, g, skip_banks[g])
            store_y(last, g, g + 1)
        for g in range(D_PASSES):
            round_y(last, g, nc.vector.tensor_copy)
        quantize_y(last - 2)
        quantize_y(last - 1)
        for g in range(D_PASSES):
            turn_y(last, g, g + 1)
            quantize_y(last, g, g + 1)
        store_scales(y_sc_late, EARLY_TILES, LATE_TILES, [nc.scalar, nc.sync])
